import numpy as np
import ml_dtypes


def mxq(x, axis, fmt="e4m3"):
    dtype, down = {"e4m3": (ml_dtypes.float8_e4m3fn, 7), "e5m2": (ml_dtypes.float8_e5m2, 14)}[fmt]
    v = np.moveaxis(np.asarray(x, np.float32).astype(ml_dtypes.bfloat16).astype(np.float64), axis, -1)
    blocks = v.reshape(v.shape[:-1] + (-1, 32))
    amax = np.abs(blocks).max(-1, keepdims=True)
    byte = np.maximum(np.where(amax > 0, np.frexp(amax)[1] - 1 + 127, 0) - down, 1)
    scale = np.exp2(byte - 127.0)
    codes = (blocks / scale).astype(np.float32).astype(dtype).astype(np.float64)
    return np.moveaxis((codes * scale).reshape(v.shape), -1, axis)


WIDE = False


def mx_kscale(k):
    if not WIDE:
        return np.ones(k)
    levels = np.array([30, -30])
    if k % 512:
        return np.exp2(np.random.permutation(np.resize(levels, k // 32))).repeat(32)
    a = np.empty((k // 512, 16))
    for p in range(k // 512):
        a[p, :8] = np.random.permutation(np.resize(levels, 8))
        for g in range(8):
            far = levels[np.abs(levels - a[p, g]) >= 10]
            a[p, g + 8] = far[np.random.randint(len(far))]
    return np.exp2(a.ravel()).repeat(32)


def f64(x):
    return np.asarray(x).astype(np.float64)


def striped(idx):
    return np.tile(np.asarray(idx).reshape(-1, 16).T, (8, 1)).astype(np.uint16)


def unstriped(offs):
    return offs[:16].T.reshape(-1).astype(np.int64)


E2M1 = np.array([0.0, 0.5, 1.0, 1.5, 2.0, 3.0, 4.0, 6.0, -0.0, -0.5, -1.0, -1.5, -2.0, -3.0, -4.0, -6.0])


def pack_weight(w, fmt):
    k, n = w.shape
    w = f64(np.asarray(w, np.float32).astype(ml_dtypes.bfloat16)).reshape(k // 32, 32, n)
    amax = np.abs(w).max(1)
    if fmt in ("e4m3", "e5m2"):
        byte = np.frexp(amax)[1] - 1 + 127 - (7 if fmt == "e4m3" else 14)
    else:
        mant, ex = np.frexp(amax / 6.0)
        byte = np.where(mant > 0.5, ex, ex - 1) + 127
    byte = np.clip(np.where(amax > 0, byte, 1), 1, 254)
    scaled = (w * np.exp2(127.0 - byte)[:, None, :]).reshape(k, n).astype(np.float32)
    by_word = np.ascontiguousarray(scaled.reshape(k // 512, 128, 4, n).transpose(0, 1, 3, 2))
    if fmt in ("e4m3", "e5m2"):
        words = by_word.astype(ml_dtypes.float8_e4m3fn if fmt == "e4m3" else ml_dtypes.float8_e5m2).view(np.uint8)
    else:
        c = by_word.astype(ml_dtypes.float4_e2m1fn).view(np.uint8) & 0xF
        words = (c[..., 0::2] | (c[..., 1::2] << 4)).reshape(k // 512, 128, 2 * n)
    return np.ascontiguousarray(words), np.ascontiguousarray(byte.astype(np.uint8).reshape(k // 512, 16, n))


def unpack_weight(words, scales, fmt):
    g, _, n = scales.shape
    words = np.ascontiguousarray(words).reshape(g, 128, n, -1)
    if fmt in ("e4m3", "e5m2"):
        vals = words.view(ml_dtypes.float8_e4m3fn if fmt == "e4m3" else ml_dtypes.float8_e5m2).astype(np.float64)
    else:
        nib = np.empty((g, 128, n, 4), np.uint8)
        nib[..., 0::2] = words & 0xF
        nib[..., 1::2] = words >> 4
        vals = E2M1[nib]
    vals = vals * np.repeat(np.exp2(scales.astype(np.float64) - 127.0), 8, axis=1)[..., None]
    return vals.transpose(0, 1, 3, 2).reshape(g * 512, n)


K, T, Z, J, R, N, L = 512, 1024, 1024, 256, 512, 256, 512


def setup_inputs():
    n = np.random.standard_normal
    idx = np.random.permutation(T)[:J]
    idx2 = np.random.permutation(Z)[:J]
    idx3 = np.random.permutation(J)[:J]
    idx4 = np.random.permutation(J)[:J]
    fk = mx_kscale(K)
    fr = mx_kscale(R)
    fl = mx_kscale(L)
    xtp = pack_weight(n((K, T)) / fk[:, None], "e2m1")
    xop = pack_weight(n((K, Z)) / fk[:, None], "e5m2")
    wp = pack_weight(n((K, R)) * 1 / np.sqrt(K) * fk[:, None] * fr, "e5m2")
    w2p = pack_weight(n((K, R)) * 1 / np.sqrt(K) * fk[:, None] * fr, "e4m3")
    wbp = pack_weight(n((R, N)) * 1 / np.sqrt(R) / fr[:, None], "e4m3")
    sxp = pack_weight(n((L, J)) / fl[:, None], "e5m2")
    wsp = pack_weight(n((L, N)) * 1 / np.sqrt(L) * fl[:, None], "e4m3")
    return {
        "xt_words": xtp[0],
        "xt_scales": xtp[1],
        "xo_words": xop[0],
        "xo_scales": xop[1],
        "w_words": wp[0],
        "w_scales": wp[1],
        "w2_words": w2p[0],
        "w2_scales": w2p[1],
        "wb_words": wbp[0],
        "wb_scales": wbp[1],
        "sx_words": sxp[0],
        "sx_scales": sxp[1],
        "ws_words": wsp[0],
        "ws_scales": wsp[1],
        "offs": striped(idx),
        "offs2": striped(idx2),
        "offs3": striped(idx3),
        "offs4": striped(idx4),
    }


def reference(xt_words, xt_scales, xo_words, xo_scales, w_words, w_scales, w2_words, w2_scales, wb_words, wb_scales, sx_words, sx_scales, ws_words, ws_scales, offs, offs2, offs3, offs4):
    idx = unstriped(offs)
    idx2 = unstriped(offs2)
    idx3 = unstriped(offs3)
    idx4 = unstriped(offs4)
    xtu = unpack_weight(xt_words, xt_scales, "e2m1")
    xou = unpack_weight(xo_words, xo_scales, "e5m2")
    wu = unpack_weight(w_words, w_scales, "e5m2")
    w2u = unpack_weight(w2_words, w2_scales, "e4m3")
    wbu = unpack_weight(wb_words, wb_scales, "e4m3")
    sxu = unpack_weight(sx_words, sx_scales, "e5m2")
    wsu = unpack_weight(ws_words, ws_scales, "e4m3")
    xtidxg = xtu[:, idx]
    xoidx2g = xou[:, idx2]
    a = wu.T @ xtidxg + w2u.T @ xoidx2g
    b = w2u.T @ xtidxg + wu.T @ xoidx2g
    hid = np.maximum(np.abs(a[:, idx3] - a[:, idx4]), b)
    hidq = mxq(hid, 0, "e5m2")
    y = wbu.T @ hidq + wsu.T @ sxu
    return y

@@ -1,0 +1,200 @@
+from contextlib import ExitStack
+
+import concourse.mybir as mybir
+
+K, T, Z, J, R, N, L = 512, 1024, 1024, 256, 512, 256, 512
+FLOPS = 2 * J * (4 * K * R + R * N + L * N)
+
+F32 = mybir.dt.float32
+BF16 = mybir.dt.bfloat16
+I32 = mybir.dt.int32
+U32 = mybir.dt.uint32
+U16 = mybir.dt.uint16
+U8 = mybir.dt.uint8
+E4M3 = mybir.dt.float8_e4m3fn_x4
+E5M2 = mybir.dt.float8_e5m2_x4
+E2M1 = mybir.dt.float4_e2m1fn_x4
+ALU = mybir.AluOpType
+ACT = mybir.ActivationFunctionType
+
+P = 128
+PACK = 4
+HALF = J // 2
+LIST_COLS = J // 16
+
+
+def load_words(queue, tile, words):
+    queue.dma_start(out=tile[:].bitcast(I32), in_=words.bitcast(I32))
+
+
+def load_scales(queue, tile, scales):
+    for q in range(4):
+        queue.dma_start(
+            out=tile[32 * q : 32 * q + 4, :].bitcast(I32),
+            in_=scales[0, 4 * q : 4 * q + 4, :].bitcast(I32),
+        )
+
+
+def fp8_rows(words):
+    return words[0].rearrange("p c t -> p (c t)")
+
+
+def tile_list_betweentwo_crossed_skip_plain_kernel(
+    tc, xt_words, xt_scales, xo_words, xo_scales, w_words, w_scales, w2_words, w2_scales,
+    wb_words, wb_scales, sx_words, sx_scales, ws_words, ws_scales, offs, offs2, offs3, offs4, out,
+):
+    nc = tc.nc
+    with ExitStack() as ctx:
+        lists = ctx.enter_context(tc.tile_pool(name="lists", bufs=1))
+        sb = ctx.enter_context(tc.tile_pool(name="sb", bufs=1))
+        psum = ctx.enter_context(tc.psum_pool(name="psum", bufs=1))
+
+        def tile(name, shape, dtype):
+            return sb.tile(shape, dtype, name=name, align_bytes=64)
+
+        idx = lists.tile([P, LIST_COLS], U16, name="idx")
+        idx2 = lists.tile([P, LIST_COLS], U16, name="idx2")
+        idx3 = lists.tile([P, LIST_COLS], U16, name="idx3")
+        idx4 = lists.tile([P, LIST_COLS], U16, name="idx4")
+
+        xt_w = tile("xt_w", [P, T], U16)
+        xt_s = tile("xt_s", [P, T], U8)
+        xo_w = tile("xo_w", [P, Z], U32)
+        xo_s = tile("xo_s", [P, Z], U8)
+        w_w = tile("w_w", [P, R], U32)
+        w_s = tile("w_s", [P, R], U8)
+        w2_w = tile("w2_w", [P, R], U32)
+        w2_s = tile("w2_s", [P, R], U8)
+        wb_w = tile("wb_w", [P, N], U32)
+        wb_s = tile("wb_s", [P, N], U8)
+        sx_w = tile("sx_w", [P, J], U32)
+        sx_s = tile("sx_s", [P, J], U8)
+        ws_w = tile("ws_w", [P, N], U32)
+        ws_s = tile("ws_s", [P, N], U8)
+
+        for plane in (xt_s, w2_s, xo_s, w_s, ws_s, sx_s, wb_s):
+            nc.vector.memset(plane[:].bitcast(I32), 0)
+
+        load_words(nc.scalar, xt_w, xt_words[0])
+        nc.sync.dma_start(idx[:], offs)
+        nc.sync.dma_start(idx2[:], offs2)
+        load_words(nc.scalar, xo_w, fp8_rows(xo_words))
+        load_scales(nc.sync, xt_s, xt_scales)
+        load_scales(nc.gpsimd, w2_s, w2_scales)
+        load_words(nc.sync, w_w, fp8_rows(w_words))
+        load_scales(nc.sync, xo_s, xo_scales)
+        load_words(nc.sync, w2_w, fp8_rows(w2_words))
+        load_scales(nc.sync, w_s, w_scales)
+        nc.sync.dma_start(idx4[:], offs4)
+        nc.sync.dma_start(idx3[:], offs3)
+        load_words(nc.sync, ws_w, fp8_rows(ws_words))
+        load_words(nc.sync, sx_w, fp8_rows(sx_words))
+        load_words(nc.sync, wb_w, fp8_rows(wb_words))
+        load_scales(nc.sync, ws_s, ws_scales)
+        load_scales(nc.sync, sx_s, sx_scales)
+        load_scales(nc.gpsimd, wb_s, wb_scales)
+
+        xtg_w = tile("xtg_w", [P, J], U16)
+        xtg_s = tile("xtg_s", [P, J], U8)
+        xog_w = tile("xog_w", [P, J], U32)
+        xog_s = tile("xog_s", [P, J], U8)
+        wp_w = tile("wp_w", [P, R], U32)
+        wp_s = tile("wp_s", [P, R], U8)
+        w2p_w = tile("w2p_w", [P, R], U32)
+        w2p_s = tile("w2p_s", [P, R], U8)
+
+        def deal_words(dst, src):
+            nc.scalar.copy(
+                out=dst[:].rearrange("p (t m) -> p m t", t=PACK),
+                in_=src[:].rearrange("p (m t) -> p m t", t=PACK),
+            )
+
+        def deal_scales(dst, src):
+            nc.vector.tensor_copy(
+                out=dst[:].rearrange("p (t m) -> p t m", t=PACK),
+                in_=src[:].rearrange("p (m t) -> p t m", t=PACK),
+            )
+
+        nc.vector.tensor_copy(xtg_w[:], xt_w[:].indirect(idx[:]))
+        nc.vector.tensor_copy(xtg_s[:], xt_s[:].indirect(idx[:]))
+        nc.vector.tensor_copy(xog_w[:], xo_w[:].indirect(idx2[:]))
+        nc.vector.tensor_copy(xog_s[:], xo_s[:].indirect(idx2[:]))
+        deal_words(wp_w, w_w)
+        deal_scales(wp_s, w_s)
+        deal_words(w2p_w, w2_w)
+        deal_scales(w2p_s, w2_s)
+
+        xt_op = (xtg_w, xtg_s, E2M1)
+        xo_op = (xog_w, xog_s, E5M2)
+        w_op = (wp_w, wp_s, E5M2)
+        w2_op = (w2p_w, w2p_s, E4M3)
+        wb_op = (wb_w, wb_s, E4M3)
+        ws_op = (ws_w, ws_s, E4M3)
+        sx_op = (sx_w, sx_s, E5M2)
+
+        def mx(acc, stationary, m0, moving, n0, n, start, stop):
+            sw, ss, sfmt = stationary
+            mw, ms, mfmt = moving
+            nc.tensor.matmul_mx(
+                out=acc,
+                lhsT=sw[:, m0 : m0 + P].bitcast(sfmt),
+                lhsT_scale=ss[:, m0 : m0 + P],
+                rhs=mw[:, n0 : n0 + n].bitcast(mfmt),
+                rhs_scale=ms[:, n0 : n0 + n],
+                start=start,
+                stop=stop,
+            )
+
+        a_ps = [psum.tile([P, J], F32, name=f"a_ps{t}") for t in range(PACK)]
+        b_ps = [psum.tile([P, PACK, HALF], F32, name=f"b_ps{h}") for h in range(2)]
+        o_ps = [psum.tile([P, 2, HALF], F32, name=f"o_ps{h}") for h in range(2)]
+
+        for t in range(PACK):
+            mx(a_ps[t][:], w_op, t * P, xt_op, 0, J, True, False)
+        for t in range(PACK):
+            mx(a_ps[t][:], w2_op, t * P, xo_op, 0, J, False, True)
+        for h in range(2):
+            for t in range(PACK):
+                mx(b_ps[h][:, t, :], w_op, t * P, xo_op, h * HALF, HALF, t == 0, False)
+        for h in range(2):
+            for t in range(PACK):
+                mx(b_ps[h][:, t, :], w2_op, t * P, xt_op, h * HALF, HALF, False, t == PACK - 1)
+        for h in range(2):
+            for g in range(2):
+                mx(o_ps[h][:, g, :], ws_op, g * P, sx_op, h * HALF, HALF, g == 0, False)
+
+        a_sb = [tile(f"a_sb{t}", [P, J], F32) for t in range(PACK)]
+        for t in range(PACK):
+            if t > 0:
+                nc.vector.tensor_copy(a_sb[t][:], a_ps[t][:])
+            else:
+                nc.scalar.copy(a_sb[t][:], a_ps[t][:])
+
+        second = [tile(f"second{h}", [P, PACK, HALF], F32) for h in range(2)]
+        diff = [tile(f"diff{h}", [P, PACK, HALF], F32) for h in range(2)]
+        mag = [tile(f"mag{h}", [P, HALF, PACK], F32) for h in range(2)]
+        hid = [tile(f"hid{h}", [P, HALF, PACK], BF16) for h in range(2)]
+        hid_w = [tile(f"hid_w{h}", [P, HALF], U32) for h in range(2)]
+        hid_s = [tile(f"hid_s{h}", [P, HALF], U8) for h in range(2)]
+        res = [tile(f"res{h}", [P, 2, HALF], F32) for h in range(2)]
+        out_rows = out.rearrange("(g p) j -> p g j", p=P)
+
+        for h in range(2):
+            cols = slice(h * LIST_COLS // 2, (h + 1) * LIST_COLS // 2)
+            for t in range(PACK):
+                nc.scalar.activation(second[h][:, t, :], a_sb[t][:].indirect(idx4[:, cols]), ACT.Copy)
+                nc.vector.tensor_tensor(
+                    diff[h][:, t, :], a_sb[t][:].indirect(idx3[:, cols]), second[h][:, t, :], ALU.subtract
+                )
+        for h in range(2):
+            nc.scalar.activation(mag[h][:], diff[h][:].rearrange("p t j -> p j t"), ACT.Abs)
+            nc.vector.tensor_tensor(hid[h][:], mag[h][:], b_ps[h][:].rearrange("p t j -> p j t"), ALU.max)
+            nc.vector.quantize_mx(
+                out=hid_w[h][:].bitcast(E5M2),
+                scales=hid_s[h][:],
+                in_=hid[h][:].rearrange("p j t -> p (j t)"),
+            )
+            for g in range(2):
+                mx(o_ps[h][:, g, :], wb_op, g * P, (hid_w[h], hid_s[h], E5M2), 0, HALF, False, g == 1)
+            nc.scalar.copy(res[h][:], o_ps[h][:])
+            nc.sync.dma_start(out=out_rows[:, :, h * HALF : (h + 1) * HALF], in_=res[h][:])

@@ -49,8 +49,8 @@ def tile_list_betweentwo_crossed_skip_plain_kernel(
         sb = ctx.enter_context(tc.tile_pool(name="sb", bufs=1))
         psum = ctx.enter_context(tc.psum_pool(name="psum", bufs=1))
 
-        def tile(name, shape, dtype):
-            return sb.tile(shape, dtype, name=name, align_bytes=64)
+        def tile(name, shape, dtype, tag=None):
+            return sb.tile(shape, dtype, name=name, tag=tag or name, align_bytes=64)
 
         idx = lists.tile([P, LIST_COLS], U16, name="idx")
         idx2 = lists.tile([P, LIST_COLS], U16, name="idx2")
@@ -65,34 +65,25 @@ def tile_list_betweentwo_crossed_skip_plain_kernel(
         w_s = tile("w_s", [P, R], U8)
         w2_w = tile("w2_w", [P, R], U32)
         w2_s = tile("w2_s", [P, R], U8)
-        wb_w = tile("wb_w", [P, N], U32)
         wb_s = tile("wb_s", [P, N], U8)
-        sx_w = tile("sx_w", [P, J], U32)
         sx_s = tile("sx_s", [P, J], U8)
-        ws_w = tile("ws_w", [P, N], U32)
         ws_s = tile("ws_s", [P, N], U8)
 
-        for plane in (xt_s, w2_s, xo_s, w_s, ws_s, sx_s, wb_s):
+        for plane in (xt_s, w_s, xo_s, w2_s, ws_s, sx_s, wb_s):
             nc.vector.memset(plane[:].bitcast(I32), 0)
 
-        load_words(nc.scalar, xt_w, xt_words[0])
+        load_words(nc.sync, xt_w, xt_words[0])
         nc.sync.dma_start(idx[:], offs)
         nc.sync.dma_start(idx2[:], offs2)
-        load_words(nc.scalar, xo_w, fp8_rows(xo_words))
+        load_words(nc.sync, xo_w, fp8_rows(xo_words))
         load_scales(nc.sync, xt_s, xt_scales)
-        load_scales(nc.gpsimd, w2_s, w2_scales)
         load_words(nc.sync, w_w, fp8_rows(w_words))
-        load_scales(nc.sync, xo_s, xo_scales)
-        load_words(nc.sync, w2_w, fp8_rows(w2_words))
         load_scales(nc.sync, w_s, w_scales)
+        load_words(nc.sync, w2_w, fp8_rows(w2_words))
+        load_scales(nc.sync, xo_s, xo_scales)
+        load_scales(nc.sync, w2_s, w2_scales)
         nc.sync.dma_start(idx4[:], offs4)
         nc.sync.dma_start(idx3[:], offs3)
-        load_words(nc.sync, ws_w, fp8_rows(ws_words))
-        load_words(nc.sync, sx_w, fp8_rows(sx_words))
-        load_words(nc.sync, wb_w, fp8_rows(wb_words))
-        load_scales(nc.sync, ws_s, ws_scales)
-        load_scales(nc.sync, sx_s, sx_scales)
-        load_scales(nc.gpsimd, wb_s, wb_scales)
 
         xtg_w = tile("xtg_w", [P, J], U16)
         xtg_s = tile("xtg_s", [P, J], U8)
@@ -109,20 +100,32 @@ def tile_list_betweentwo_crossed_skip_plain_kernel(
                 in_=src[:].rearrange("p (m t) -> p m t", t=PACK),
             )
 
-        def deal_scales(dst, src):
+        def deal_scales(dst, src, t0, t1):
             nc.vector.tensor_copy(
-                out=dst[:].rearrange("p (t m) -> p t m", t=PACK),
-                in_=src[:].rearrange("p (m t) -> p t m", t=PACK),
+                out=dst[:].rearrange("p (t m) -> p t m", t=PACK)[:, t0:t1, :],
+                in_=src[:].rearrange("p (m t) -> p t m", t=PACK)[:, t0:t1, :],
             )
 
         nc.vector.tensor_copy(xtg_w[:], xt_w[:].indirect(idx[:]))
         nc.vector.tensor_copy(xtg_s[:], xt_s[:].indirect(idx[:]))
         nc.vector.tensor_copy(xog_w[:], xo_w[:].indirect(idx2[:]))
-        nc.vector.tensor_copy(xog_s[:], xo_s[:].indirect(idx2[:]))
         deal_words(wp_w, w_w)
-        deal_scales(wp_s, w_s)
+        deal_scales(wp_s, w_s, 0, PACK)
+        nc.vector.tensor_copy(xog_s[:], xo_s[:].indirect(idx2[:]))
         deal_words(w2p_w, w2_w)
-        deal_scales(w2p_s, w2_s)
+        deal_scales(w2p_s, w2_s, 0, 1)
+        deal_scales(w2p_s, w2_s, 1, PACK)
+
+        skip_w = tile("skip_w", [P, N + J], U32, tag="w_w")
+        ws_w = skip_w[:, 0:N]
+        sx_w = skip_w[:, N : N + J]
+        wb_w = tile("wb_w", [P, N], U32, tag="w2_w")
+        load_scales(nc.sync, ws_s, ws_scales)
+        load_scales(nc.sync, sx_s, sx_scales)
+        load_words(nc.sync, ws_w, fp8_rows(ws_words))
+        load_words(nc.sync, sx_w, fp8_rows(sx_words))
+        load_words(nc.sync, wb_w, fp8_rows(wb_words))
+        load_scales(nc.sync, wb_s, wb_scales)
 
         xt_op = (xtg_w, xtg_s, E2M1)
         xo_op = (xog_w, xog_s, E5M2)
@@ -145,9 +148,8 @@ def tile_list_betweentwo_crossed_skip_plain_kernel(
                 stop=stop,
             )
 
-        a_ps = [psum.tile([P, J], F32, name=f"a_ps{t}") for t in range(PACK)]
+        a_ps = [psum.tile([P, J], F32, name=f"a_ps{t}", tag=f"a_ps{t}") for t in range(PACK)]
         b_ps = [psum.tile([P, PACK, HALF], F32, name=f"b_ps{h}") for h in range(2)]
-        o_ps = [psum.tile([P, 2, HALF], F32, name=f"o_ps{h}") for h in range(2)]
 
         for t in range(PACK):
             mx(a_ps[t][:], w_op, t * P, xt_op, 0, J, True, False)
@@ -159,42 +161,60 @@ def tile_list_betweentwo_crossed_skip_plain_kernel(
         for h in range(2):
             for t in range(PACK):
                 mx(b_ps[h][:, t, :], w2_op, t * P, xt_op, h * HALF, HALF, False, t == PACK - 1)
+        a_sb = [tile(f"a_sb{t}", [P, 2 * J], F32) for t in range(PACK)]
+        for t in range(PACK):
+            nc.gpsimd.memset(a_sb[t][:, J:], 0.0)
+
+        second = tile("second", [P, PACK, J], F32)
+        diff = tile("diff", [P, PACK, J], F32)
+
+        def look_up(t, j0, j1):
+            cols = slice(j0 // 16, j1 // 16)
+            nc.scalar.activation(second[:, t, j0:j1], a_sb[t][:].indirect(idx4[:, cols]), ACT.Copy)
+            nc.vector.tensor_tensor(
+                diff[:, t, j0:j1], a_sb[t][:].indirect(idx3[:, cols]), second[:, t, j0:j1], ALU.subtract
+            )
+
+        nc.scalar.copy(a_sb[0][:, 0:J], a_ps[0][:])
+        nc.vector.tensor_copy(a_sb[1][:, 0:J], a_ps[1][:])
+        nc.vector.tensor_copy(a_sb[2][:, 0:J], a_ps[2][:])
+        look_up(0, 0, J)
+        look_up(1, 0, J)
+        nc.vector.tensor_copy(a_sb[3][:, 0:J], a_ps[3][:])
+        look_up(2, 0, J)
+        look_up(3, 0, HALF)
+        look_up(3, HALF, J)
+
+        o_ps = {}
         for h in range(2):
             for g in range(2):
-                mx(o_ps[h][:, g, :], ws_op, g * P, sx_op, h * HALF, HALF, g == 0, False)
+                o_ps[h, g] = psum.tile([P, HALF], F32, name=f"o_ps{h}{g}", tag=f"a_ps{2 * h + g}")
+                mx(o_ps[h, g][:], ws_op, g * P, sx_op, h * HALF, HALF, True, False)
 
-        a_sb = [tile(f"a_sb{t}", [P, J], F32) for t in range(PACK)]
-        for t in range(PACK):
-            if t > 0:
-                nc.vector.tensor_copy(a_sb[t][:], a_ps[t][:])
-            else:
-                nc.scalar.copy(a_sb[t][:], a_ps[t][:])
-
-        second = [tile(f"second{h}", [P, PACK, HALF], F32) for h in range(2)]
-        diff = [tile(f"diff{h}", [P, PACK, HALF], F32) for h in range(2)]
         mag = [tile(f"mag{h}", [P, HALF, PACK], F32) for h in range(2)]
         hid = [tile(f"hid{h}", [P, HALF, PACK], BF16) for h in range(2)]
         hid_w = [tile(f"hid_w{h}", [P, HALF], U32) for h in range(2)]
         hid_s = [tile(f"hid_s{h}", [P, HALF], U8) for h in range(2)]
-        res = [tile(f"res{h}", [P, 2, HALF], F32) for h in range(2)]
-        out_rows = out.rearrange("(g p) j -> p g j", p=P)
+        diff_jt = diff[:].rearrange("p t j -> p j t")
 
+        for h, j0, j1 in ((0, 0, HALF // 2), (0, HALF // 2, HALF), (1, 0, HALF)):
+            nc.scalar.activation(mag[h][:, j0:j1, :], diff_jt[:, h * HALF + j0 : h * HALF + j1, :], ACT.Abs)
+            nc.vector.tensor_tensor(
+                hid[h][:, j0:j1, :], mag[h][:, j0:j1, :], b_ps[h][:].rearrange("p t j -> p j t")[:, j0:j1, :], ALU.max
+            )
         for h in range(2):
-            cols = slice(h * LIST_COLS // 2, (h + 1) * LIST_COLS // 2)
-            for t in range(PACK):
-                nc.scalar.activation(second[h][:, t, :], a_sb[t][:].indirect(idx4[:, cols]), ACT.Copy)
-                nc.vector.tensor_tensor(
-                    diff[h][:, t, :], a_sb[t][:].indirect(idx3[:, cols]), second[h][:, t, :], ALU.subtract
-                )
-        for h in range(2):
-            nc.scalar.activation(mag[h][:], diff[h][:].rearrange("p t j -> p j t"), ACT.Abs)
-            nc.vector.tensor_tensor(hid[h][:], mag[h][:], b_ps[h][:].rearrange("p t j -> p j t"), ALU.max)
             nc.vector.quantize_mx(
                 out=hid_w[h][:].bitcast(E5M2),
                 scales=hid_s[h][:],
                 in_=hid[h][:].rearrange("p j t -> p (j t)"),
             )
             for g in range(2):
-                mx(o_ps[h][:, g, :], wb_op, g * P, (hid_w[h], hid_s[h], E5M2), 0, HALF, False, g == 1)
-            nc.scalar.copy(res[h][:], o_ps[h][:])
-            nc.sync.dma_start(out=out_rows[:, :, h * HALF : (h + 1) * HALF], in_=res[h][:])
+                mx(o_ps[h, g][:], wb_op, g * P, (hid_w[h], hid_s[h], E5M2), 0, HALF, False, True)
+                res = tile(f"res{h}{g}", [P, HALF], F32)
+                rows = out[g * P : (g + 1) * P, h * HALF : (h + 1) * HALF]
+                if h == 1 and g == 1:
+                    nc.vector.tensor_copy(res[:], o_ps[h, g][:])
+                    nc.sync.dma_start(out=rows, in_=res[:])
+                else:
+                    nc.scalar.copy(res[:], o_ps[h, g][:])
+                    (nc.scalar if h == 1 else nc.sync).dma_start(out=rows, in_=res[:])

@@ -28,10 +28,10 @@ def load_words(queue, tile, words):
 
 
 def load_scales(queue, tile, scales):
-    for q in range(4):
+    for r in range(4):
         queue.dma_start(
-            out=tile[32 * q : 32 * q + 4, :].bitcast(I32),
-            in_=scales[0, 4 * q : 4 * q + 4, :].bitcast(I32),
+            out=tile[r:P:32, :].bitcast(I32),
+            in_=scales[0, r:16:4, :].bitcast(I32),
         )
 
 
@@ -69,17 +69,17 @@ def tile_list_betweentwo_crossed_skip_plain_kernel(
         sx_s = tile("sx_s", [P, J], U8)
         ws_s = tile("ws_s", [P, N], U8)
 
-        for plane in (xt_s, w_s, xo_s, w2_s, ws_s, sx_s, wb_s):
+        for plane in (w_s, xt_s, xo_s, w2_s, ws_s, sx_s, wb_s):
             nc.vector.memset(plane[:].bitcast(I32), 0)
 
         load_words(nc.sync, xt_w, xt_words[0])
+        load_words(nc.scalar, xo_w, fp8_rows(xo_words))
         nc.sync.dma_start(idx[:], offs)
+        load_words(nc.scalar, w_w, fp8_rows(w_words))
         nc.sync.dma_start(idx2[:], offs2)
-        load_words(nc.sync, xo_w, fp8_rows(xo_words))
-        load_scales(nc.sync, xt_s, xt_scales)
-        load_words(nc.sync, w_w, fp8_rows(w_words))
+        load_words(nc.scalar, w2_w, fp8_rows(w2_words))
         load_scales(nc.sync, w_s, w_scales)
-        load_words(nc.sync, w2_w, fp8_rows(w2_words))
+        load_scales(nc.sync, xt_s, xt_scales)
         load_scales(nc.sync, xo_s, xo_scales)
         load_scales(nc.sync, w2_s, w2_scales)
         nc.sync.dma_start(idx4[:], offs4)
@@ -96,8 +96,8 @@ def tile_list_betweentwo_crossed_skip_plain_kernel(
 
         def deal_words(dst, src):
             nc.scalar.copy(
-                out=dst[:].rearrange("p (t m) -> p m t", t=PACK),
-                in_=src[:].rearrange("p (m t) -> p m t", t=PACK),
+                out=dst[:].rearrange("p (t c i) -> p c t i", t=PACK, i=4),
+                in_=src[:].rearrange("p (c i t) -> p c t i", t=PACK, i=4),
             )
 
         def deal_scales(dst, src, t0, t1):
@@ -107,10 +107,10 @@ def tile_list_betweentwo_crossed_skip_plain_kernel(
             )
 
         nc.vector.tensor_copy(xtg_w[:], xt_w[:].indirect(idx[:]))
-        nc.vector.tensor_copy(xtg_s[:], xt_s[:].indirect(idx[:]))
         nc.vector.tensor_copy(xog_w[:], xo_w[:].indirect(idx2[:]))
         deal_words(wp_w, w_w)
         deal_scales(wp_s, w_s, 0, PACK)
+        nc.vector.tensor_copy(xtg_s[:], xt_s[:].indirect(idx[:]))
         nc.vector.tensor_copy(xog_s[:], xo_s[:].indirect(idx2[:]))
         deal_words(w2p_w, w2_w)
         deal_scales(w2p_s, w2_s, 0, 1)
@@ -157,10 +157,10 @@ def tile_list_betweentwo_crossed_skip_plain_kernel(
             mx(a_ps[t][:], w2_op, t * P, xo_op, 0, J, False, True)
         for h in range(2):
             for t in range(PACK):
-                mx(b_ps[h][:, t, :], w_op, t * P, xo_op, h * HALF, HALF, t == 0, False)
+                mx(b_ps[h][:, t, :], w2_op, t * P, xt_op, h * HALF, HALF, t == 0, False)
         for h in range(2):
             for t in range(PACK):
-                mx(b_ps[h][:, t, :], w2_op, t * P, xt_op, h * HALF, HALF, False, t == PACK - 1)
+                mx(b_ps[h][:, t, :], w_op, t * P, xo_op, h * HALF, HALF, False, t == PACK - 1)
         a_sb = [tile(f"a_sb{t}", [P, 2 * J], F32) for t in range(PACK)]
         for t in range(PACK):
             nc.gpsimd.memset(a_sb[t][:, J:], 0.0)

from contextlib import ExitStack

import concourse.mybir as mybir

K, T, Z, J, R, N, L = 512, 1024, 1024, 256, 512, 256, 512
FLOPS = 2 * J * (4 * K * R + R * N + L * N)

F32 = mybir.dt.float32
BF16 = mybir.dt.bfloat16
I32 = mybir.dt.int32
U32 = mybir.dt.uint32
U16 = mybir.dt.uint16
U8 = mybir.dt.uint8
E4M3 = mybir.dt.float8_e4m3fn_x4
E5M2 = mybir.dt.float8_e5m2_x4
E2M1 = mybir.dt.float4_e2m1fn_x4
ALU = mybir.AluOpType
ACT = mybir.ActivationFunctionType

P = 128
PACK = 4
HALF = J // 2
LIST_COLS = J // 16


def load_words(queue, tile, words):
    queue.dma_start(out=tile[:].bitcast(I32), in_=words.bitcast(I32))


def load_scales(queue, tile, scales):
    for r in range(4):
        queue.dma_start(
            out=tile[r:P:32, :].bitcast(I32),
            in_=scales[0, r:16:4, :].bitcast(I32),
        )


def fp8_rows(words):
    return words[0].rearrange("p c t -> p (c t)")


def tile_list_betweentwo_crossed_skip_plain_kernel(
    tc, xt_words, xt_scales, xo_words, xo_scales, w_words, w_scales, w2_words, w2_scales,
    wb_words, wb_scales, sx_words, sx_scales, ws_words, ws_scales, offs, offs2, offs3, offs4, out,
):
    nc = tc.nc
    with ExitStack() as ctx:
        lists = ctx.enter_context(tc.tile_pool(name="lists", bufs=1))
        sb = ctx.enter_context(tc.tile_pool(name="sb", bufs=1))
        psum = ctx.enter_context(tc.psum_pool(name="psum", bufs=1))

        def tile(name, shape, dtype, tag=None):
            return sb.tile(shape, dtype, name=name, tag=tag or name, align_bytes=64)

        idx = lists.tile([P, LIST_COLS], U16, name="idx")
        idx2 = lists.tile([P, LIST_COLS], U16, name="idx2")
        idx3 = lists.tile([P, LIST_COLS], U16, name="idx3")
        idx4 = lists.tile([P, LIST_COLS], U16, name="idx4")

        xt_w = tile("xt_w", [P, T], U16)
        xt_s = tile("xt_s", [P, T], U8)
        xo_w = tile("xo_w", [P, Z], U32)
        xo_s = tile("xo_s", [P, Z], U8)
        w_w = tile("w_w", [P, R], U32)
        w_s = tile("w_s", [P, R], U8)
        w2_w = tile("w2_w", [P, R], U32)
        w2_s = tile("w2_s", [P, R], U8)
        wb_s = tile("wb_s", [P, N], U8)
        sx_s = tile("sx_s", [P, J], U8)
        ws_s = tile("ws_s", [P, N], U8)

        for plane in (w_s, xt_s, xo_s, w2_s, ws_s, sx_s, wb_s):
            nc.vector.memset(plane[:].bitcast(I32), 0)

        load_words(nc.sync, xt_w, xt_words[0])
        load_words(nc.scalar, xo_w, fp8_rows(xo_words))
        nc.sync.dma_start(idx[:], offs)
        load_words(nc.scalar, w_w, fp8_rows(w_words))
        nc.sync.dma_start(idx2[:], offs2)
        load_words(nc.scalar, w2_w, fp8_rows(w2_words))
        load_scales(nc.sync, w_s, w_scales)
        load_scales(nc.sync, xt_s, xt_scales)
        load_scales(nc.sync, xo_s, xo_scales)
        load_scales(nc.sync, w2_s, w2_scales)
        nc.sync.dma_start(idx4[:], offs4)
        nc.sync.dma_start(idx3[:], offs3)

        xtg_w = tile("xtg_w", [P, J], U16)
        xtg_s = tile("xtg_s", [P, J], U8)
        xog_w = tile("xog_w", [P, J], U32)
        xog_s = tile("xog_s", [P, J], U8)
        wp_w = tile("wp_w", [P, R], U32)
        wp_s = tile("wp_s", [P, R], U8)
        w2p_w = tile("w2p_w", [P, R], U32)
        w2p_s = tile("w2p_s", [P, R], U8)

        def deal_words(dst, src):
            nc.scalar.copy(
                out=dst[:].rearrange("p (t c i) -> p c t i", t=PACK, i=4),
                in_=src[:].rearrange("p (c i t) -> p c t i", t=PACK, i=4),
            )

        def deal_scales(dst, src, t0, t1):
            nc.vector.tensor_copy(
                out=dst[:].rearrange("p (t m) -> p t m", t=PACK)[:, t0:t1, :],
                in_=src[:].rearrange("p (m t) -> p t m", t=PACK)[:, t0:t1, :],
            )

        nc.vector.tensor_copy(xtg_w[:], xt_w[:].indirect(idx[:]))
        nc.vector.tensor_copy(xog_w[:], xo_w[:].indirect(idx2[:]))
        deal_words(wp_w, w_w)
        deal_scales(wp_s, w_s, 0, PACK)
        nc.vector.tensor_copy(xtg_s[:], xt_s[:].indirect(idx[:]))
        nc.vector.tensor_copy(xog_s[:], xo_s[:].indirect(idx2[:]))
        deal_words(w2p_w, w2_w)
        deal_scales(w2p_s, w2_s, 0, 1)
        deal_scales(w2p_s, w2_s, 1, PACK)

        skip_w = tile("skip_w", [P, N + J], U32, tag="w_w")
        ws_w = skip_w[:, 0:N]
        sx_w = skip_w[:, N : N + J]
        wb_w = tile("wb_w", [P, N], U32, tag="w2_w")
        load_scales(nc.sync, ws_s, ws_scales)
        load_scales(nc.sync, sx_s, sx_scales)
        load_words(nc.sync, ws_w, fp8_rows(ws_words))
        load_words(nc.sync, sx_w, fp8_rows(sx_words))
        load_words(nc.sync, wb_w, fp8_rows(wb_words))
        load_scales(nc.sync, wb_s, wb_scales)

        xt_op = (xtg_w, xtg_s, E2M1)
        xo_op = (xog_w, xog_s, E5M2)
        w_op = (wp_w, wp_s, E5M2)
        w2_op = (w2p_w, w2p_s, E4M3)
        wb_op = (wb_w, wb_s, E4M3)
        ws_op = (ws_w, ws_s, E4M3)
        sx_op = (sx_w, sx_s, E5M2)

        def mx(acc, stationary, m0, moving, n0, n, start, stop):
            sw, ss, sfmt = stationary
            mw, ms, mfmt = moving
            nc.tensor.matmul_mx(
                out=acc,
                lhsT=sw[:, m0 : m0 + P].bitcast(sfmt),
                lhsT_scale=ss[:, m0 : m0 + P],
                rhs=mw[:, n0 : n0 + n].bitcast(mfmt),
                rhs_scale=ms[:, n0 : n0 + n],
                start=start,
                stop=stop,
            )

        a_ps = [psum.tile([P, J], F32, name=f"a_ps{t}", tag=f"a_ps{t}") for t in range(PACK)]
        b_ps = [psum.tile([P, PACK, HALF], F32, name=f"b_ps{h}") for h in range(2)]

        for t in range(PACK):
            mx(a_ps[t][:], w_op, t * P, xt_op, 0, J, True, False)
        for t in range(PACK):
            mx(a_ps[t][:], w2_op, t * P, xo_op, 0, J, False, True)
        for h in range(2):
            for t in range(PACK):
                mx(b_ps[h][:, t, :], w2_op, t * P, xt_op, h * HALF, HALF, t == 0, False)
        for h in range(2):
            for t in range(PACK):
                mx(b_ps[h][:, t, :], w_op, t * P, xo_op, h * HALF, HALF, False, t == PACK - 1)
        a_sb = [tile(f"a_sb{t}", [P, 2 * J], F32) for t in range(PACK)]
        for t in range(PACK):
            nc.gpsimd.memset(a_sb[t][:, J:], 0.0)

        second = tile("second", [P, PACK, J], F32)
        diff = tile("diff", [P, PACK, J], F32)

        def look_up(t, j0, j1):
            cols = slice(j0 // 16, j1 // 16)
            nc.scalar.activation(second[:, t, j0:j1], a_sb[t][:].indirect(idx4[:, cols]), ACT.Copy)
            nc.vector.tensor_tensor(
                diff[:, t, j0:j1], a_sb[t][:].indirect(idx3[:, cols]), second[:, t, j0:j1], ALU.subtract
            )

        nc.scalar.copy(a_sb[0][:, 0:J], a_ps[0][:])
        nc.vector.tensor_copy(a_sb[1][:, 0:J], a_ps[1][:])
        nc.vector.tensor_copy(a_sb[2][:, 0:J], a_ps[2][:])
        look_up(0, 0, J)
        look_up(1, 0, J)
        nc.vector.tensor_copy(a_sb[3][:, 0:J], a_ps[3][:])
        look_up(2, 0, J)
        look_up(3, 0, HALF)
        look_up(3, HALF, J)

        o_ps = {}
        for h in range(2):
            for g in range(2):
                o_ps[h, g] = psum.tile([P, HALF], F32, name=f"o_ps{h}{g}", tag=f"a_ps{2 * h + g}")
                mx(o_ps[h, g][:], ws_op, g * P, sx_op, h * HALF, HALF, True, False)

        mag = [tile(f"mag{h}", [P, HALF, PACK], F32) for h in range(2)]
        hid = [tile(f"hid{h}", [P, HALF, PACK], BF16) for h in range(2)]
        hid_w = [tile(f"hid_w{h}", [P, HALF], U32) for h in range(2)]
        hid_s = [tile(f"hid_s{h}", [P, HALF], U8) for h in range(2)]
        diff_jt = diff[:].rearrange("p t j -> p j t")

        for h, j0, j1 in ((0, 0, HALF // 2), (0, HALF // 2, HALF), (1, 0, HALF)):
            nc.scalar.activation(mag[h][:, j0:j1, :], diff_jt[:, h * HALF + j0 : h * HALF + j1, :], ACT.Abs)
            nc.vector.tensor_tensor(
                hid[h][:, j0:j1, :], mag[h][:, j0:j1, :], b_ps[h][:].rearrange("p t j -> p j t")[:, j0:j1, :], ALU.max
            )
        for h in range(2):
            nc.vector.quantize_mx(
                out=hid_w[h][:].bitcast(E5M2),
                scales=hid_s[h][:],
                in_=hid[h][:].rearrange("p j t -> p (j t)"),
            )
            for g in range(2):
                mx(o_ps[h, g][:], wb_op, g * P, (hid_w[h], hid_s[h], E5M2), 0, HALF, False, True)
                res = tile(f"res{h}{g}", [P, HALF], F32)
                rows = out[g * P : (g + 1) * P, h * HALF : (h + 1) * HALF]
                if h == 1 and g == 1:
                    nc.vector.tensor_copy(res[:], o_ps[h, g][:])
                    nc.sync.dma_start(out=rows, in_=res[:])
                else:
                    nc.scalar.copy(res[:], o_ps[h, g][:])
                    (nc.scalar if h == 1 else nc.sync).dma_start(out=rows, in_=res[:])
